import numpy as np
import ml_dtypes


def mxq(x, axis, fmt="e4m3"):
    dtype, down = {"e4m3": (ml_dtypes.float8_e4m3fn, 7), "e5m2": (ml_dtypes.float8_e5m2, 14)}[fmt]
    v = np.moveaxis(np.asarray(x, np.float32).astype(ml_dtypes.bfloat16).astype(np.float64), axis, -1)
    blocks = v.reshape(v.shape[:-1] + (-1, 32))
    amax = np.abs(blocks).max(-1, keepdims=True)
    byte = np.maximum(np.where(amax > 0, np.frexp(amax)[1] - 1 + 127, 0) - down, 1)
    scale = np.exp2(byte - 127.0)
    codes = (blocks / scale).astype(np.float32).astype(dtype).astype(np.float64)
    return np.moveaxis((codes * scale).reshape(v.shape), -1, axis)


WIDE = False


def mx_kscale(k):
    if not WIDE:
        return np.ones(k)
    levels = np.array([10, -10, 5, -5, 0])
    if k % 512:
        return np.exp2(np.random.permutation(np.resize(levels, k // 32))).repeat(32)
    a = np.empty((k // 512, 16))
    for p in range(k // 512):
        a[p, :8] = np.random.permutation(np.resize(levels, 8))
        for g in range(8):
            far = levels[np.abs(levels - a[p, g]) >= 10]
            a[p, g + 8] = far[np.random.randint(len(far))]
    return np.exp2(a.ravel()).repeat(32)


def f64(x):
    return np.asarray(x).astype(np.float64)


def striped(idx):
    return np.tile(idx.reshape(-1, 16).T, (8, 1)).astype(np.uint16)


def unstriped(offs):
    return offs[:16].T.reshape(-1).astype(np.int64)


def pack_weight(w):
    k, n = w.shape
    w = f64(np.asarray(w, np.float32).astype(ml_dtypes.bfloat16)).reshape(k // 32, 32, n)
    amax = np.abs(w).max(1)
    byte = np.clip(np.where(amax > 0, np.frexp(amax)[1] - 1 + 127 - 7, 1), 1, 254)
    scaled = (w * np.exp2(127.0 - byte)[:, None, :]).reshape(k, n).astype(np.float32)
    words = np.ascontiguousarray(scaled.reshape(k // 512, 128, 4, n).transpose(0, 1, 3, 2)).astype(ml_dtypes.float8_e4m3fn).view(np.uint8)
    return words, np.ascontiguousarray(byte.astype(np.uint8).reshape(k // 512, 16, n))


def unpack_weight(words, scales):
    g, p, n, _ = words.shape
    vals = np.ascontiguousarray(words).view(ml_dtypes.float8_e4m3fn).astype(np.float64) * np.repeat(np.exp2(scales.astype(np.float64) - 127.0), 8, axis=1)[..., None]
    return vals.transpose(0, 1, 3, 2).reshape(g * 512, n)

def planes(y):
    n, m = y.shape
    v = y.astype(np.float32).astype(ml_dtypes.bfloat16).astype(np.float64).reshape(n // 32, 32, m)
    top = np.abs(v).max(1)
    byte = np.clip(np.where(top > 0, np.frexp(top)[1] - 1 + 127 - 7, 1), 1, 254)
    codes = (v * np.exp2(127.0 - byte)[:, None, :]).reshape(n, m).astype(np.float32).astype(ml_dtypes.float8_e4m3fn).view(np.uint8)
    words = codes.reshape(n // 512, 128, 4, m).transpose(0, 1, 3, 2)
    return np.ascontiguousarray(words), np.ascontiguousarray(byte.astype(np.uint8).reshape(n // 512, 16, m))


K, T, N, U = 512, 512, 512, 1024


def setup_inputs():
    n = np.random.standard_normal
    s = mx_kscale(K)[:, None]
    packed_xT = pack_weight(n((K, T)) * s)
    return {
        "x_words": packed_xT[0],
        "x_scales": packed_xT[1],
        "mem": n((N, U)).astype(np.float32),
        "w1": (n((K, N)) / np.sqrt(K) / s).astype(np.float32),
        "slot": striped(np.random.permutation(U)[:T]),
    }


def reference(x_words, x_scales, mem, w1, slot):
    xq = unpack_weight(x_words, x_scales)
    y = mxq(f64(w1), 0, "e4m3").T @ xq
    out = f64(mem).copy()
    out[:, unstriped(slot)] = f64(mem)[:, unstriped(slot)] + y
    return (out,) + planes(out)

@@ -1,0 +1,125 @@
+from contextlib import ExitStack
+
+import concourse.mybir as mybir
+
+K, T, N, U = 512, 512, 512, 1024
+FLOPS = 2 * K * T * N
+
+F32 = mybir.dt.float32
+BF16 = mybir.dt.bfloat16
+I32 = mybir.dt.int32
+U32 = mybir.dt.uint32
+U16 = mybir.dt.uint16
+U8 = mybir.dt.uint8
+FP8X4 = mybir.dt.float8_e4m3fn_x4
+ADD = mybir.AluOpType.add
+
+P = 128
+PACK = 4
+PARTS = ((0, 512), (512, 768), (768, 1024))
+ORDER = (2, 0, 1, 3)
+
+
+def tile_picked_widxput_add_lo_kernel(tc, x_words, x_scales, mem, w1, slot, out_0, out_1, out_2):
+    nc = tc.nc
+    mem_rows = mem.rearrange("(p t) u -> p t u", t=PACK)
+    out_rows = out_0.rearrange("(p t) u -> p t u", t=PACK)
+    w_rows = w1.rearrange("(p j) n -> p j n", j=PACK)
+    out_words = out_1[0].rearrange("p u r -> p (u r)").bitcast(I32)
+    out_scales = out_2[0].bitcast(I32)
+    x_scale_rows = x_scales[0].bitcast(I32)
+
+    with ExitStack() as ctx:
+        keep = ctx.enter_context(tc.tile_pool(name="keep", bufs=1))
+        ring = ctx.enter_context(tc.tile_pool(name="ring", bufs=2))
+        ring3 = ctx.enter_context(tc.tile_pool(name="ring3", bufs=3))
+        psum = ctx.enter_context(tc.psum_pool(name="psum", bufs=1))
+
+        offsets = keep.tile([P, T // 16], U16, name="offsets")
+        x_codes = keep.tile([P, T], U32, name="x_codes", align_bytes=64)
+        x_plane = keep.tile([P, T], U8, name="x_plane", align_bytes=64)
+        half = N // 2
+        w_raw = [keep.tile([P, PACK, half], F32, name=f"w_raw{h}") for h in range(2)]
+        w_grouped = keep.tile([P, N * PACK], BF16, name="w_grouped", align_bytes=64)
+        w_codes = keep.tile([P, N], U32, name="w_codes", align_bytes=64)
+        w_plane = keep.tile([P, N], U8, name="w_plane", align_bytes=64)
+        store = [keep.tile([P, U], F32, name=f"store{t}") for t in range(PACK)]
+        grouped = [keep.tile([P, (b - a) * PACK], BF16, name=f"grouped{a}", align_bytes=64) for a, b in PARTS]
+        codes = [keep.tile([P, b - a], U32, name=f"codes{a}", align_bytes=64) for a, b in PARTS]
+        plane = keep.tile([P, U], U8, name="plane", align_bytes=64)
+
+        nc.vector.memset(x_plane[:].bitcast(I32), 0)
+        nc.sync.dma_start(offsets[:], slot)
+        nc.sync.dma_start(out=store[ORDER[0]][:], in_=mem_rows[:, ORDER[0], :])
+        nc.sync.dma_start(out=x_plane[0 : 4, :].bitcast(I32), in_=x_scale_rows[0 : 4, :])
+        nc.sync.dma_start(out=x_plane[32 : 36, :].bitcast(I32), in_=x_scale_rows[4 : 8, :])
+        nc.sync.dma_start(out=x_plane[64 : 68, :].bitcast(I32), in_=x_scale_rows[8 : 12, :])
+        nc.sync.dma_start(out=x_plane[96 : 100, :].bitcast(I32), in_=x_scale_rows[12 : 16, :])
+        nc.sync.dma_start(out=w_raw[0][:], in_=w_rows[:, :, 0:half])
+        nc.sync.dma_start(out=w_raw[1][:], in_=w_rows[:, :, half:N])
+        nc.sync.dma_start(out=x_codes[:].bitcast(I32), in_=x_words[0].rearrange("p n r -> p (n r)").bitcast(I32))
+        nc.sync.dma_start(out=store[ORDER[1]][:], in_=mem_rows[:, ORDER[1], :])
+        nc.sync.dma_start(out=store[ORDER[2]][:], in_=mem_rows[:, ORDER[2], :])
+        nc.sync.dma_start(out=store[ORDER[3]][:], in_=mem_rows[:, ORDER[3], :])
+
+        dealt = w_grouped[:].rearrange("p (t m j) -> p m j t", t=PACK, j=PACK)
+        for h in range(2):
+            nc.vector.tensor_copy(
+                out=dealt[:, h * (P // 2) : (h + 1) * (P // 2)],
+                in_=w_raw[h][:].rearrange("p j (m t) -> p m j t", t=PACK),
+            )
+        for a, b in ((2 * P, 3 * P), (0, 2 * P), (3 * P, 4 * P)):
+            nc.vector.quantize_mx(out=w_codes[:, a:b].bitcast(FP8X4), scales=w_plane[:, a:b], in_=w_grouped[:, PACK * a : PACK * b])
+
+        acc = {}
+        for t in ORDER:
+            acc[t] = psum.tile([P, T], F32, name=f"acc{t}")
+            nc.tensor.matmul_mx(
+                out=acc[t][:],
+                lhsT=w_codes[:, t * P : (t + 1) * P].bitcast(FP8X4),
+                lhsT_scale=w_plane[:, t * P : (t + 1) * P],
+                rhs=x_codes[:].bitcast(FP8X4),
+                rhs_scale=x_plane[:],
+                start=True,
+                stop=True,
+            )
+
+        update = {}
+        old = {}
+
+        def fetch(t, name):
+            update[t] = ring3.tile([P, T], F32, name="update")
+            nc.scalar.copy(out=update[t][:], in_=acc[t][:])
+
+        def gather(t):
+            old[t] = ring.tile([P, T], F32, name="old")
+            nc.vector.tensor_copy(old[t][:], store[t][:].indirect(offsets[:]))
+
+        def regroup(copy, t, i):
+            a, b = PARTS[i]
+            copy(out=grouped[i][:].rearrange("p (u r) -> p u r", r=PACK)[:, :, t], in_=store[t][:, a:b])
+
+        for t in ORDER[:-1]:
+            fetch(t, f"update{t}")
+        gather(ORDER[0])
+        for s, t in enumerate(ORDER):
+            if s + 1 < PACK:
+                gather(ORDER[s + 1])
+            nc.vector.tensor_tensor(store[t][:].indirect(offsets[:]), old[t][:], update[t][:], ADD)
+            nc.sync.dma_start(out=out_rows[:, t, :], in_=store[t][:])
+            if s + 1 < PACK:
+                for i in range(len(PARTS)):
+                    regroup(nc.scalar.copy, t, i)
+                    if s == 0 and i == 0:
+                        fetch(ORDER[-1], "")
+        last = PACK - 1
+        regroup(nc.vector.tensor_copy, last, 0)
+        regroup(nc.scalar.copy, last, 1)
+        regroup(nc.scalar.copy, last, 2)
+        for i in (1, 0, 2):
+            a, b = PARTS[i]
+            nc.vector.quantize_mx(out=codes[i][:].bitcast(FP8X4), scales=plane[:, a:b], in_=grouped[i][:])
+            nc.sync.dma_start(out=out_words[:, a:b], in_=codes[i][:].bitcast(I32))
+        for q in range(4):
+            queue = nc.scalar if q % 2 else nc.sync
+            queue.dma_start(out=out_scales[4 * q : 4 * q + 4, :], in_=plane[32 * q : 32 * q + 4, :].bitcast(I32))

@@ -93,11 +93,15 @@ def tile_picked_widxput_add_lo_kernel(tc, x_words, x_scales, mem, w1, slot, out_
 
         def gather(t):
             old[t] = ring.tile([P, T], F32, name="old")
-            nc.vector.tensor_copy(old[t][:], store[t][:].indirect(offsets[:]))
+            if t in ORDER[:2]:
+                nc.vector.tensor_copy(old[t][:], store[t][:].indirect(offsets[:]))
+            else:
+                nc.vector.tensor_tensor(old[t][:], store[t][:].indirect(offsets[:]), update[t][:], ADD)
 
-        def regroup(copy, t, i):
+        def regroup(copy, t, i, lo=0, hi=None):
             a, b = PARTS[i]
-            copy(out=grouped[i][:].rearrange("p (u r) -> p u r", r=PACK)[:, :, t], in_=store[t][:, a:b])
+            hi = b - a if hi is None else hi
+            copy(out=grouped[i][:].rearrange("p (u r) -> p u r", r=PACK)[:, lo:hi, t], in_=store[t][:, a + lo : a + hi])
 
         for t in ORDER[:-1]:
             fetch(t, f"update{t}")
@@ -105,18 +109,22 @@ def tile_picked_widxput_add_lo_kernel(tc, x_words, x_scales, mem, w1, slot, out_
         for s, t in enumerate(ORDER):
             if s + 1 < PACK:
                 gather(ORDER[s + 1])
-            nc.vector.tensor_tensor(store[t][:].indirect(offsets[:]), old[t][:], update[t][:], ADD)
+            if t in ORDER[:2]:
+                nc.vector.tensor_tensor(store[t][:].indirect(offsets[:]), old[t][:], update[t][:], ADD)
+            else:
+                nc.vector.tensor_copy(store[t][:].indirect(offsets[:]), old[t][:])
             nc.sync.dma_start(out=out_rows[:, t, :], in_=store[t][:])
             if s + 1 < PACK:
                 for i in range(len(PARTS)):
                     regroup(nc.scalar.copy, t, i)
-                    if s == 0 and i == 0:
+                    if s == 0 and i == len(PARTS) - 1:
                         fetch(ORDER[-1], "")
         last = PACK - 1
         regroup(nc.vector.tensor_copy, last, 0)
+        regroup(nc.vector.tensor_copy, last, 2, 0, 64)
         regroup(nc.scalar.copy, last, 1)
-        regroup(nc.scalar.copy, last, 2)
-        for i in (1, 0, 2):
+        regroup(nc.scalar.copy, last, 2, 64)
+        for i in (0, 1, 2):
             a, b = PARTS[i]
             nc.vector.quantize_mx(out=codes[i][:].bitcast(FP8X4), scales=plane[:, a:b], in_=grouped[i][:])
             nc.sync.dma_start(out=out_words[:, a:b], in_=codes[i][:].bitcast(I32))

@@ -48,13 +48,11 @@ def tile_picked_widxput_add_lo_kernel(tc, x_words, x_scales, mem, w1, slot, out_
         codes = [keep.tile([P, b - a], U32, name=f"codes{a}", align_bytes=64) for a, b in PARTS]
         plane = keep.tile([P, U], U8, name="plane", align_bytes=64)
 
-        nc.vector.memset(x_plane[:].bitcast(I32), 0)
-        nc.sync.dma_start(offsets[:], slot)
+        nc.gpsimd.memset(x_plane[:].bitcast(I32), 0)
+        for q in range(4):
+            nc.gpsimd.dma_start(out=x_plane[32 * q : 32 * q + 4, :].bitcast(I32), in_=x_scale_rows[4 * q : 4 * q + 4, :])
         nc.sync.dma_start(out=store[ORDER[0]][:], in_=mem_rows[:, ORDER[0], :])
-        nc.sync.dma_start(out=x_plane[0 : 4, :].bitcast(I32), in_=x_scale_rows[0 : 4, :])
-        nc.sync.dma_start(out=x_plane[32 : 36, :].bitcast(I32), in_=x_scale_rows[4 : 8, :])
-        nc.sync.dma_start(out=x_plane[64 : 68, :].bitcast(I32), in_=x_scale_rows[8 : 12, :])
-        nc.sync.dma_start(out=x_plane[96 : 100, :].bitcast(I32), in_=x_scale_rows[12 : 16, :])
+        nc.sync.dma_start(offsets[:], slot)
         nc.sync.dma_start(out=w_raw[0][:], in_=w_rows[:, :, 0:half])
         nc.sync.dma_start(out=w_raw[1][:], in_=w_rows[:, :, half:N])
         nc.sync.dma_start(out=x_codes[:].bitcast(I32), in_=x_words[0].rearrange("p n r -> p (n r)").bitcast(I32))
@@ -93,10 +91,7 @@ def tile_picked_widxput_add_lo_kernel(tc, x_words, x_scales, mem, w1, slot, out_
 
         def gather(t):
             old[t] = ring.tile([P, T], F32, name="old")
-            if t in ORDER[:2]:
-                nc.vector.tensor_copy(old[t][:], store[t][:].indirect(offsets[:]))
-            else:
-                nc.vector.tensor_tensor(old[t][:], store[t][:].indirect(offsets[:]), update[t][:], ADD)
+            nc.vector.tensor_copy(old[t][:], store[t][:].indirect(offsets[:]))
 
         def regroup(copy, t, i, lo=0, hi=None):
             a, b = PARTS[i]
@@ -109,10 +104,7 @@ def tile_picked_widxput_add_lo_kernel(tc, x_words, x_scales, mem, w1, slot, out_
         for s, t in enumerate(ORDER):
             if s + 1 < PACK:
                 gather(ORDER[s + 1])
-            if t in ORDER[:2]:
-                nc.vector.tensor_tensor(store[t][:].indirect(offsets[:]), old[t][:], update[t][:], ADD)
-            else:
-                nc.vector.tensor_copy(store[t][:].indirect(offsets[:]), old[t][:])
+            nc.vector.tensor_tensor(store[t][:].indirect(offsets[:]), old[t][:], update[t][:], ADD)
             nc.sync.dma_start(out=out_rows[:, t, :], in_=store[t][:])
             if s + 1 < PACK:
                 for i in range(len(PARTS)):

@@ -16,7 +16,9 @@ ADD = mybir.AluOpType.add
 
 P = 128
 PACK = 4
-PARTS = ((0, 512), (512, 768), (768, 1024))
+PARTS = ((0, 256), (768, 1024), (256, 512), (512, 768))
+ON_VECTOR = ((0, 256), (256, 576))
+ON_SCALAR = ((768, 1024), (576, 768))
 ORDER = (2, 0, 1, 3)
 
 
@@ -44,15 +46,17 @@ def tile_picked_widxput_add_lo_kernel(tc, x_words, x_scales, mem, w1, slot, out_
         w_codes = keep.tile([P, N], U32, name="w_codes", align_bytes=64)
         w_plane = keep.tile([P, N], U8, name="w_plane", align_bytes=64)
         store = [keep.tile([P, U], F32, name=f"store{t}") for t in range(PACK)]
-        grouped = [keep.tile([P, (b - a) * PACK], BF16, name=f"grouped{a}", align_bytes=64) for a, b in PARTS]
+        grouped = keep.tile([P, U * PACK], BF16, name="grouped", align_bytes=64)
         codes = [keep.tile([P, b - a], U32, name=f"codes{a}", align_bytes=64) for a, b in PARTS]
         plane = keep.tile([P, U], U8, name="plane", align_bytes=64)
 
-        nc.gpsimd.memset(x_plane[:].bitcast(I32), 0)
-        for q in range(4):
-            nc.gpsimd.dma_start(out=x_plane[32 * q : 32 * q + 4, :].bitcast(I32), in_=x_scale_rows[4 * q : 4 * q + 4, :])
-        nc.sync.dma_start(out=store[ORDER[0]][:], in_=mem_rows[:, ORDER[0], :])
+        nc.vector.memset(x_plane[:].bitcast(I32), 0)
         nc.sync.dma_start(offsets[:], slot)
+        nc.sync.dma_start(out=store[ORDER[0]][:], in_=mem_rows[:, ORDER[0], :])
+        nc.sync.dma_start(out=x_plane[0 : 4, :].bitcast(I32), in_=x_scale_rows[0 : 4, :])
+        nc.sync.dma_start(out=x_plane[32 : 36, :].bitcast(I32), in_=x_scale_rows[4 : 8, :])
+        nc.sync.dma_start(out=x_plane[64 : 68, :].bitcast(I32), in_=x_scale_rows[8 : 12, :])
+        nc.sync.dma_start(out=x_plane[96 : 100, :].bitcast(I32), in_=x_scale_rows[12 : 16, :])
         nc.sync.dma_start(out=w_raw[0][:], in_=w_rows[:, :, 0:half])
         nc.sync.dma_start(out=w_raw[1][:], in_=w_rows[:, :, half:N])
         nc.sync.dma_start(out=x_codes[:].bitcast(I32), in_=x_words[0].rearrange("p n r -> p (n r)").bitcast(I32))
@@ -71,32 +75,35 @@ def tile_picked_widxput_add_lo_kernel(tc, x_words, x_scales, mem, w1, slot, out_
 
         acc = {}
         for t in ORDER:
-            acc[t] = psum.tile([P, T], F32, name=f"acc{t}")
-            nc.tensor.matmul_mx(
-                out=acc[t][:],
-                lhsT=w_codes[:, t * P : (t + 1) * P].bitcast(FP8X4),
-                lhsT_scale=w_plane[:, t * P : (t + 1) * P],
-                rhs=x_codes[:].bitcast(FP8X4),
-                rhs_scale=x_plane[:],
-                start=True,
-                stop=True,
-            )
+            pieces = ((0, T // 2), (T // 2, T)) if t == ORDER[0] else ((0, T),)
+            acc[t] = []
+            for a, b in pieces:
+                bank = psum.tile([P, b - a], F32, name=f"acc{t}_{a}")
+                nc.tensor.matmul_mx(
+                    out=bank[:],
+                    lhsT=w_codes[:, t * P : (t + 1) * P].bitcast(FP8X4),
+                    lhsT_scale=w_plane[:, t * P : (t + 1) * P],
+                    rhs=x_codes[:, a:b].bitcast(FP8X4),
+                    rhs_scale=x_plane[:, a:b],
+                    start=True,
+                    stop=True,
+                )
+                acc[t].append((a, b, bank))
 
         update = {}
         old = {}
 
         def fetch(t, name):
             update[t] = ring3.tile([P, T], F32, name="update")
-            nc.scalar.copy(out=update[t][:], in_=acc[t][:])
+            for a, b, bank in acc[t]:
+                nc.scalar.copy(out=update[t][:, a:b], in_=bank[:])
 
         def gather(t):
             old[t] = ring.tile([P, T], F32, name="old")
             nc.vector.tensor_copy(old[t][:], store[t][:].indirect(offsets[:]))
 
-        def regroup(copy, t, i, lo=0, hi=None):
-            a, b = PARTS[i]
-            hi = b - a if hi is None else hi
-            copy(out=grouped[i][:].rearrange("p (u r) -> p u r", r=PACK)[:, lo:hi, t], in_=store[t][:, a + lo : a + hi])
+        def regroup(copy, t, a, b):
+            copy(out=grouped[:].rearrange("p (u r) -> p u r", r=PACK)[:, a:b, t], in_=store[t][:, a:b])
 
         for t in ORDER[:-1]:
             fetch(t, f"update{t}")
@@ -107,18 +114,16 @@ def tile_picked_widxput_add_lo_kernel(tc, x_words, x_scales, mem, w1, slot, out_
             nc.vector.tensor_tensor(store[t][:].indirect(offsets[:]), old[t][:], update[t][:], ADD)
             nc.sync.dma_start(out=out_rows[:, t, :], in_=store[t][:])
             if s + 1 < PACK:
-                for i in range(len(PARTS)):
-                    regroup(nc.scalar.copy, t, i)
-                    if s == 0 and i == len(PARTS) - 1:
-                        fetch(ORDER[-1], "")
+                regroup(nc.scalar.copy, t, 0, U)
+            if s == 0:
+                fetch(ORDER[-1], "")
         last = PACK - 1
-        regroup(nc.vector.tensor_copy, last, 0)
-        regroup(nc.vector.tensor_copy, last, 2, 0, 64)
-        regroup(nc.scalar.copy, last, 1)
-        regroup(nc.scalar.copy, last, 2, 64)
-        for i in (0, 1, 2):
-            a, b = PARTS[i]
-            nc.vector.quantize_mx(out=codes[i][:].bitcast(FP8X4), scales=plane[:, a:b], in_=grouped[i][:])
+        for a, b in ON_VECTOR:
+            regroup(nc.vector.tensor_copy, last, a, b)
+        for a, b in ON_SCALAR:
+            regroup(nc.scalar.copy, last, a, b)
+        for i, (a, b) in enumerate(PARTS):
+            nc.vector.quantize_mx(out=codes[i][:].bitcast(FP8X4), scales=plane[:, a:b], in_=grouped[:, PACK * a : PACK * b])
             nc.sync.dma_start(out=out_words[:, a:b], in_=codes[i][:].bitcast(I32))
         for q in range(4):
             queue = nc.scalar if q % 2 else nc.sync

@@ -16,10 +16,12 @@ ADD = mybir.AluOpType.add
 
 P = 128
 PACK = 4
-PARTS = ((0, 256), (768, 1024), (256, 512), (512, 768))
-ON_VECTOR = ((0, 256), (256, 576))
-ON_SCALAR = ((768, 1024), (576, 768))
+CAST_SPLIT = 108
+STORES = (((0, 256), (256, 512)), ((512, 768),), ((768, 896), (896, 1024)))
+ON_VECTOR = ((0, 256), (512, 768))
+ON_SCALAR = ((256, 512), (768, 896), (896, 1024))
 ORDER = (2, 0, 1, 3)
+EARLY = 128
 
 
 def tile_picked_widxput_add_lo_kernel(tc, x_words, x_scales, mem, w1, slot, out_0, out_1, out_2):
@@ -27,104 +29,136 @@ def tile_picked_widxput_add_lo_kernel(tc, x_words, x_scales, mem, w1, slot, out_
     mem_rows = mem.rearrange("(p t) u -> p t u", t=PACK)
     out_rows = out_0.rearrange("(p t) u -> p t u", t=PACK)
     w_rows = w1.rearrange("(p j) n -> p j n", j=PACK)
+    x_rows = x_words[0].rearrange("p n r -> p (n r)").bitcast(I32)
     out_words = out_1[0].rearrange("p u r -> p (u r)").bitcast(I32)
     out_scales = out_2[0].bitcast(I32)
     x_scale_rows = x_scales[0].bitcast(I32)
+    half = N // 2
+    first, second, third, last = ORDER
 
     with ExitStack() as ctx:
         keep = ctx.enter_context(tc.tile_pool(name="keep", bufs=1))
-        ring = ctx.enter_context(tc.tile_pool(name="ring", bufs=2))
-        ring3 = ctx.enter_context(tc.tile_pool(name="ring3", bufs=3))
+        ring = ctx.enter_context(tc.tile_pool(name="ring", bufs=3))
         psum = ctx.enter_context(tc.psum_pool(name="psum", bufs=1))
 
         offsets = keep.tile([P, T // 16], U16, name="offsets")
         x_codes = keep.tile([P, T], U32, name="x_codes", align_bytes=64)
         x_plane = keep.tile([P, T], U8, name="x_plane", align_bytes=64)
-        half = N // 2
-        w_raw = [keep.tile([P, PACK, half], F32, name=f"w_raw{h}") for h in range(2)]
-        w_grouped = keep.tile([P, N * PACK], BF16, name="w_grouped", align_bytes=64)
-        w_codes = keep.tile([P, N], U32, name="w_codes", align_bytes=64)
         w_plane = keep.tile([P, N], U8, name="w_plane", align_bytes=64)
+        w_raw = [keep.tile([P, PACK, half], F32, name=f"w_raw{h}", tag=f"w_raw{h}", align_bytes=64) for h in range(2)]
+        w_grouped = keep.tile([P, N * PACK], BF16, name="w_grouped", tag="w_grouped", align_bytes=64)
+        w_codes = keep.tile([P, N], U32, name="w_codes", align_bytes=64)
         store = [keep.tile([P, U], F32, name=f"store{t}") for t in range(PACK)]
         grouped = keep.tile([P, U * PACK], BF16, name="grouped", align_bytes=64)
-        codes = [keep.tile([P, b - a], U32, name=f"codes{a}", align_bytes=64) for a, b in PARTS]
+        codes = [keep.tile([P, parts[-1][1] - parts[0][0]], U32, name=f"codes{parts[0][0]}", align_bytes=64) for parts in STORES]
         plane = keep.tile([P, U], U8, name="plane", align_bytes=64)
 
+        def load_w(h):
+            nc.sync.dma_start(out=w_raw[h][:], in_=w_rows[:, :, h * half : (h + 1) * half])
+
+        def load_x(a, b):
+            nc.sync.dma_start(out=x_codes[:, a:b].bitcast(I32), in_=x_rows[:, a:b])
+
+        def load_mem(t):
+            nc.sync.dma_start(out=store[t][:], in_=mem_rows[:, t, :])
+
+        def load_scales(queue):
+            for q in range(4):
+                queue.dma_start(out=x_plane[32 * q : 32 * q + 4, :].bitcast(I32), in_=x_scale_rows[4 * q : 4 * q + 4, :])
+
         nc.vector.memset(x_plane[:].bitcast(I32), 0)
+        load_w(0)
+        load_w(1)
         nc.sync.dma_start(offsets[:], slot)
-        nc.sync.dma_start(out=store[ORDER[0]][:], in_=mem_rows[:, ORDER[0], :])
-        nc.sync.dma_start(out=x_plane[0 : 4, :].bitcast(I32), in_=x_scale_rows[0 : 4, :])
-        nc.sync.dma_start(out=x_plane[32 : 36, :].bitcast(I32), in_=x_scale_rows[4 : 8, :])
-        nc.sync.dma_start(out=x_plane[64 : 68, :].bitcast(I32), in_=x_scale_rows[8 : 12, :])
-        nc.sync.dma_start(out=x_plane[96 : 100, :].bitcast(I32), in_=x_scale_rows[12 : 16, :])
-        nc.sync.dma_start(out=w_raw[0][:], in_=w_rows[:, :, 0:half])
-        nc.sync.dma_start(out=w_raw[1][:], in_=w_rows[:, :, half:N])
-        nc.sync.dma_start(out=x_codes[:].bitcast(I32), in_=x_words[0].rearrange("p n r -> p (n r)").bitcast(I32))
-        nc.sync.dma_start(out=store[ORDER[1]][:], in_=mem_rows[:, ORDER[1], :])
-        nc.sync.dma_start(out=store[ORDER[2]][:], in_=mem_rows[:, ORDER[2], :])
-        nc.sync.dma_start(out=store[ORDER[3]][:], in_=mem_rows[:, ORDER[3], :])
-
-        dealt = w_grouped[:].rearrange("p (t m j) -> p m j t", t=PACK, j=PACK)
-        for h in range(2):
-            nc.vector.tensor_copy(
-                out=dealt[:, h * (P // 2) : (h + 1) * (P // 2)],
-                in_=w_raw[h][:].rearrange("p j (m t) -> p m j t", t=PACK),
-            )
-        for a, b in ((2 * P, 3 * P), (0, 2 * P), (3 * P, 4 * P)):
-            nc.vector.quantize_mx(out=w_codes[:, a:b].bitcast(FP8X4), scales=w_plane[:, a:b], in_=w_grouped[:, PACK * a : PACK * b])
-
-        acc = {}
-        for t in ORDER:
-            pieces = ((0, T // 2), (T // 2, T)) if t == ORDER[0] else ((0, T),)
-            acc[t] = []
-            for a, b in pieces:
-                bank = psum.tile([P, b - a], F32, name=f"acc{t}_{a}")
-                nc.tensor.matmul_mx(
-                    out=bank[:],
-                    lhsT=w_codes[:, t * P : (t + 1) * P].bitcast(FP8X4),
-                    lhsT_scale=w_plane[:, t * P : (t + 1) * P],
-                    rhs=x_codes[:, a:b].bitcast(FP8X4),
-                    rhs_scale=x_plane[:, a:b],
-                    start=True,
-                    stop=True,
-                )
-                acc[t].append((a, b, bank))
+        load_mem(first)
+        load_mem(second)
+        load_scales(nc.sync)
+        load_x(0, EARLY)
+        load_mem(third)
+        load_x(EARLY, T)
+        load_mem(last)
 
         update = {}
         old = {}
+        acc = {}
 
-        def fetch(t, name):
-            update[t] = ring3.tile([P, T], F32, name="update")
+        def cast(copy, a, b):
+            h = a // (P // 2)
+            dealt = w_grouped[:].rearrange("p (t m j) -> p m j t", t=PACK, j=PACK)
+            raw = w_raw[h][:].rearrange("p j (m t) -> p m j t", t=PACK)
+            copy(out=dealt[:, a:b], in_=raw[:, a - h * (P // 2) : b - h * (P // 2)])
+
+        def gather(t, tag):
+            old[t] = keep.tile([P, T], F32, name=f"old{t}", tag=tag, align_bytes=64)
+            nc.vector.tensor_copy(old[t][:], store[t][:].indirect(offsets[:]))
+
+        def multiply(t, a, b, bank):
+            nc.tensor.matmul_mx(
+                out=bank,
+                lhsT=w_codes[:, t * P : (t + 1) * P].bitcast(FP8X4),
+                lhsT_scale=w_plane[:, t * P : (t + 1) * P],
+                rhs=x_codes[:, a:b].bitcast(FP8X4),
+                rhs_scale=x_plane[:, a:b],
+                start=True,
+                stop=True,
+            )
+
+        def fetch(t):
+            update[t] = ring.tile([P, T], F32, name="update")
             for a, b, bank in acc[t]:
                 nc.scalar.copy(out=update[t][:, a:b], in_=bank[:])
 
-        def gather(t):
-            old[t] = ring.tile([P, T], F32, name="old")
-            nc.vector.tensor_copy(old[t][:], store[t][:].indirect(offsets[:]))
+        def put(t, a, b):
+            nc.vector.tensor_tensor(store[t][:].indirect(offsets[:, a // 16 : b // 16]), old[t][:, a:b], update[t][:, a:b], ADD)
+
+        def scatter(t, a=0):
+            put(t, a, T)
+            nc.sync.dma_start(out=out_rows[:, t, :], in_=store[t][:])
 
         def regroup(copy, t, a, b):
             copy(out=grouped[:].rearrange("p (u r) -> p u r", r=PACK)[:, a:b, t], in_=store[t][:, a:b])
 
-        for t in ORDER[:-1]:
-            fetch(t, f"update{t}")
-        gather(ORDER[0])
-        for s, t in enumerate(ORDER):
-            if s + 1 < PACK:
-                gather(ORDER[s + 1])
-            nc.vector.tensor_tensor(store[t][:].indirect(offsets[:]), old[t][:], update[t][:], ADD)
-            nc.sync.dma_start(out=out_rows[:, t, :], in_=store[t][:])
-            if s + 1 < PACK:
-                regroup(nc.scalar.copy, t, 0, U)
-            if s == 0:
-                fetch(ORDER[-1], "")
-        last = PACK - 1
+        cast(nc.vector.tensor_copy, 0, P // 2)
+        cast(nc.vector.tensor_copy, P // 2, CAST_SPLIT)
+        cast(nc.scalar.copy, CAST_SPLIT, P)
+        nc.vector.quantize_mx(out=w_codes[:].bitcast(FP8X4), scales=w_plane[:], in_=w_grouped[:])
+
+        early = psum.tile([P, EARLY], F32, name="acc_early")
+        late = psum.tile([P, T - EARLY], F32, name="acc_late")
+        acc[first] = [(0, EARLY, early), (EARLY, T, late)]
+        multiply(first, 0, EARLY, early[:])
+        multiply(first, EARLY, half, late[:, 0 : half - EARLY])
+        multiply(first, half, T, late[:, half - EARLY : T - EARLY])
+        for t in ORDER[1:]:
+            bank = psum.tile([P, T], F32, name=f"acc{t}")
+            acc[t] = [(0, T, bank)]
+            multiply(t, 0, T, bank[:])
+
+        gather(first, "w_raw1")
+        gather(second, "w_grouped")
+        fetch(first)
+        fetch(second)
+        fetch(third)
+        put(first, 0, EARLY)
+        gather(third, "old_third")
+        scatter(first, EARLY)
+        regroup(nc.scalar.copy, first, 0, U)
+        fetch(last)
+        scatter(second)
+        gather(last, "w_raw1")
+        regroup(nc.scalar.copy, second, 0, U)
+        scatter(third)
+        regroup(nc.scalar.copy, third, 0, U)
+        scatter(last)
         for a, b in ON_VECTOR:
             regroup(nc.vector.tensor_copy, last, a, b)
         for a, b in ON_SCALAR:
             regroup(nc.scalar.copy, last, a, b)
-        for i, (a, b) in enumerate(PARTS):
-            nc.vector.quantize_mx(out=codes[i][:].bitcast(FP8X4), scales=plane[:, a:b], in_=grouped[:, PACK * a : PACK * b])
-            nc.sync.dma_start(out=out_words[:, a:b], in_=codes[i][:].bitcast(I32))
+        for i, parts in enumerate(STORES):
+            start = parts[0][0]
+            for a, b in parts:
+                nc.vector.quantize_mx(out=codes[i][:, a - start : b - start].bitcast(FP8X4), scales=plane[:, a:b], in_=grouped[:, PACK * a : PACK * b])
+            nc.sync.dma_start(out=out_words[:, start : parts[-1][1]], in_=codes[i][:].bitcast(I32))
         for q in range(4):
             queue = nc.scalar if q % 2 else nc.sync
             queue.dma_start(out=out_scales[4 * q : 4 * q + 4, :], in_=plane[32 * q : 32 * q + 4, :].bitcast(I32))

@@ -13,15 +13,16 @@ U16 = mybir.dt.uint16
 U8 = mybir.dt.uint8
 FP8X4 = mybir.dt.float8_e4m3fn_x4
 ADD = mybir.AluOpType.add
+COPY = mybir.ActivationFunctionType.Copy
 
 P = 128
 PACK = 4
 CAST_SPLIT = 108
+LATE = 128
+LEAD = 128
+ON_VECTOR = ((0, 256), (256, 576))
+ON_SCALAR = ((576, 768), (768, 1024))
 STORES = (((0, 256), (256, 512)), ((512, 768),), ((768, 896), (896, 1024)))
-ON_VECTOR = ((0, 256), (512, 768))
-ON_SCALAR = ((256, 512), (768, 896), (896, 1024))
-ORDER = (2, 0, 1, 3)
-EARLY = 128
 
 
 def tile_picked_widxput_add_lo_kernel(tc, x_words, x_scales, mem, w1, slot, out_0, out_1, out_2):
@@ -33,53 +34,48 @@ def tile_picked_widxput_add_lo_kernel(tc, x_words, x_scales, mem, w1, slot, out_
     out_words = out_1[0].rearrange("p u r -> p (u r)").bitcast(I32)
     out_scales = out_2[0].bitcast(I32)
     x_scale_rows = x_scales[0].bitcast(I32)
-    half = N // 2
-    first, second, third, last = ORDER
+    half = T // 2
+    front, back = (0, half), (half, T)
 
     with ExitStack() as ctx:
         keep = ctx.enter_context(tc.tile_pool(name="keep", bufs=1))
-        ring = ctx.enter_context(tc.tile_pool(name="ring", bufs=3))
         psum = ctx.enter_context(tc.psum_pool(name="psum", bufs=1))
 
         offsets = keep.tile([P, T // 16], U16, name="offsets")
         x_codes = keep.tile([P, T], U32, name="x_codes", align_bytes=64)
         x_plane = keep.tile([P, T], U8, name="x_plane", align_bytes=64)
         w_plane = keep.tile([P, N], U8, name="w_plane", align_bytes=64)
-        w_raw = [keep.tile([P, PACK, half], F32, name=f"w_raw{h}", tag=f"w_raw{h}", align_bytes=64) for h in range(2)]
-        w_grouped = keep.tile([P, N * PACK], BF16, name="w_grouped", tag="w_grouped", align_bytes=64)
+        w_raw = [keep.tile([P, PACK, N // 2], F32, name=f"w_raw{h}", align_bytes=64) for h in range(2)]
+        w_grouped = keep.tile([P, N * PACK], BF16, name="w_grouped", align_bytes=64)
         w_codes = keep.tile([P, N], U32, name="w_codes", align_bytes=64)
         store = [keep.tile([P, U], F32, name=f"store{t}") for t in range(PACK)]
+        old = [keep.tile([P, T], F32, name=f"old{t}") for t in range(PACK)]
+        fresh = [keep.tile([P, T], F32, name=f"fresh{t}") for t in range(PACK)]
+        stage = {(a, b): keep.tile([P, PACK, b - a], F32, name=f"stage{a}", align_bytes=64) for a, b in ON_VECTOR + ON_SCALAR}
         grouped = keep.tile([P, U * PACK], BF16, name="grouped", align_bytes=64)
         codes = [keep.tile([P, parts[-1][1] - parts[0][0]], U32, name=f"codes{parts[0][0]}", align_bytes=64) for parts in STORES]
         plane = keep.tile([P, U], U8, name="plane", align_bytes=64)
 
-        def load_w(h):
-            nc.sync.dma_start(out=w_raw[h][:], in_=w_rows[:, :, h * half : (h + 1) * half])
-
         def load_x(a, b):
             nc.sync.dma_start(out=x_codes[:, a:b].bitcast(I32), in_=x_rows[:, a:b])
 
-        def load_mem(t):
-            nc.sync.dma_start(out=store[t][:], in_=mem_rows[:, t, :])
-
-        def load_scales(queue):
-            for q in range(4):
-                queue.dma_start(out=x_plane[32 * q : 32 * q + 4, :].bitcast(I32), in_=x_scale_rows[4 * q : 4 * q + 4, :])
+        def load_mem(t, a, b):
+            nc.sync.dma_start(out=store[t][:, a:b], in_=mem_rows[:, t, a:b])
 
         nc.vector.memset(x_plane[:].bitcast(I32), 0)
-        load_w(0)
-        load_w(1)
+        for h in range(2):
+            nc.sync.dma_start(out=w_raw[h][:], in_=w_rows[:, :, h * (N // 2) : (h + 1) * (N // 2)])
         nc.sync.dma_start(offsets[:], slot)
-        load_mem(first)
-        load_mem(second)
-        load_scales(nc.sync)
-        load_x(0, EARLY)
-        load_mem(third)
-        load_x(EARLY, T)
-        load_mem(last)
+        load_mem(0, 0, U)
+        for q in range(4):
+            nc.sync.dma_start(out=x_plane[32 * q : 32 * q + 4, :].bitcast(I32), in_=x_scale_rows[4 * q : 4 * q + 4, :])
+        load_x(*front)
+        load_mem(1, 0, U)
+        load_x(*back)
+        load_mem(3, 0, U - LATE)
+        load_mem(2, 0, U)
+        load_mem(3, U - LATE, U)
 
-        update = {}
-        old = {}
         acc = {}
 
         def cast(copy, a, b):
@@ -88,13 +84,10 @@ def tile_picked_widxput_add_lo_kernel(tc, x_words, x_scales, mem, w1, slot, out_
             raw = w_raw[h][:].rearrange("p j (m t) -> p m j t", t=PACK)
             copy(out=dealt[:, a:b], in_=raw[:, a - h * (P // 2) : b - h * (P // 2)])
 
-        def gather(t, tag):
-            old[t] = keep.tile([P, T], F32, name=f"old{t}", tag=tag, align_bytes=64)
-            nc.vector.tensor_copy(old[t][:], store[t][:].indirect(offsets[:]))
-
-        def multiply(t, a, b, bank):
+        def multiply(t, a, b):
+            acc[t, a] = psum.tile([P, b - a], F32, name=f"acc{t}_{a}")
             nc.tensor.matmul_mx(
-                out=bank,
+                out=acc[t, a][:],
                 lhsT=w_codes[:, t * P : (t + 1) * P].bitcast(FP8X4),
                 lhsT_scale=w_plane[:, t * P : (t + 1) * P],
                 rhs=x_codes[:, a:b].bitcast(FP8X4),
@@ -103,57 +96,85 @@ def tile_picked_widxput_add_lo_kernel(tc, x_words, x_scales, mem, w1, slot, out_
                 stop=True,
             )
 
-        def fetch(t):
-            update[t] = ring.tile([P, T], F32, name="update")
-            for a, b, bank in acc[t]:
-                nc.scalar.copy(out=update[t][:, a:b], in_=bank[:])
+        def picked(t, a, b):
+            return store[t][:].indirect(offsets[:, a // 16 : b // 16])
 
-        def put(t, a, b):
-            nc.vector.tensor_tensor(store[t][:].indirect(offsets[:, a // 16 : b // 16]), old[t][:, a:b], update[t][:, a:b], ADD)
+        def gather_on_scalar(t, a, b):
+            nc.scalar.activation(old[t][:, a:b], picked(t, a, b), COPY)
 
-        def scatter(t, a=0):
-            put(t, a, T)
+        def add(t, a, b, sums):
+            nc.vector.tensor_tensor(fresh[t][:, a:b], old[t][:, a:b], sums, ADD)
+
+        def scatter_on_scalar(t, a, b):
+            nc.scalar.activation(picked(t, a, b), fresh[t][:, a:b], COPY)
+
+        def fetch(copy, t, a, b):
+            copy(out=fresh[t][:, a:b], in_=acc[t, a][:])
+
+        def scatter_sum(t):
+            nc.vector.tensor_tensor(picked(t, 0, T), old[t][:], fresh[t][:], ADD)
+
+        def hand_on(t):
             nc.sync.dma_start(out=out_rows[:, t, :], in_=store[t][:])
 
-        def regroup(copy, t, a, b):
-            copy(out=grouped[:].rearrange("p (u r) -> p u r", r=PACK)[:, a:b, t], in_=store[t][:, a:b])
+        def move(copy, t, part):
+            a, b = part
+            copy(out=stage[part][:, t, :], in_=store[t][:, a:b])
+
+        def interleave(copy, part, a, b):
+            first = part[0]
+            copy(
+                out=grouped[:, PACK * a : PACK * b].rearrange("p (c i t) -> p c t i", i=4, t=PACK),
+                in_=stage[part][:, :, a - first : b - first].rearrange("p t (c i) -> p c t i", i=4),
+            )
 
         cast(nc.vector.tensor_copy, 0, P // 2)
         cast(nc.vector.tensor_copy, P // 2, CAST_SPLIT)
         cast(nc.scalar.copy, CAST_SPLIT, P)
         nc.vector.quantize_mx(out=w_codes[:].bitcast(FP8X4), scales=w_plane[:], in_=w_grouped[:])
 
-        early = psum.tile([P, EARLY], F32, name="acc_early")
-        late = psum.tile([P, T - EARLY], F32, name="acc_late")
-        acc[first] = [(0, EARLY, early), (EARLY, T, late)]
-        multiply(first, 0, EARLY, early[:])
-        multiply(first, EARLY, half, late[:, 0 : half - EARLY])
-        multiply(first, half, T, late[:, half - EARLY : T - EARLY])
-        for t in ORDER[1:]:
-            bank = psum.tile([P, T], F32, name=f"acc{t}")
-            acc[t] = [(0, T, bank)]
-            multiply(t, 0, T, bank[:])
+        for t in (0, 1, 3, 2):
+            multiply(t, *front)
+        for t in (1, 0, 3, 2):
+            multiply(t, *back)
 
-        gather(first, "w_raw1")
-        gather(second, "w_grouped")
-        fetch(first)
-        fetch(second)
-        fetch(third)
-        put(first, 0, EARLY)
-        gather(third, "old_third")
-        scatter(first, EARLY)
-        regroup(nc.scalar.copy, first, 0, U)
-        fetch(last)
-        scatter(second)
-        gather(last, "w_raw1")
-        regroup(nc.scalar.copy, second, 0, U)
-        scatter(third)
-        regroup(nc.scalar.copy, third, 0, U)
-        scatter(last)
-        for a, b in ON_VECTOR:
-            regroup(nc.vector.tensor_copy, last, a, b)
-        for a, b in ON_SCALAR:
-            regroup(nc.scalar.copy, last, a, b)
+        gather_on_scalar(0, *front)
+        gather_on_scalar(0, *back)
+        add(0, *front, acc[0, 0][:])
+        fetch(nc.scalar.copy, 1, *front)
+        scatter_on_scalar(0, *front)
+        fetch(nc.vector.tensor_copy, 3, *front)
+        nc.vector.tensor_copy(old[1][:], picked(1, 0, T))
+        fetch(nc.scalar.copy, 1, *back)
+        add(0, *back, acc[0, half][:])
+        scatter_on_scalar(0, *back)
+        fetch(nc.vector.tensor_copy, 3, *back)
+        scatter_sum(1)
+        for t in range(2):
+            for part in stage:
+                move(nc.sync.dma_start, t, part)
+            hand_on(t)
+        gather_on_scalar(2, 0, T)
+        gather_on_scalar(3, 0, T)
+        add(2, 0, LEAD, acc[2, 0][:, 0:LEAD])
+        add(2, LEAD, half, acc[2, 0][:, LEAD:half])
+        add(2, *back, acc[2, half][:])
+        scatter_on_scalar(2, 0, LEAD)
+        scatter_on_scalar(2, LEAD, T)
+        scatter_sum(3)
+        hand_on(3)
+        hand_on(2)
+        for t in (3, 2):
+            for part in ON_VECTOR:
+                move(nc.vector.tensor_copy, t, part)
+            for part in ON_SCALAR:
+                move(nc.scalar.copy, t, part)
+
+        for part in ON_VECTOR:
+            interleave(nc.vector.tensor_copy, part, *part)
+        interleave(nc.scalar.copy, ON_SCALAR[0], *ON_SCALAR[0])
+        interleave(nc.scalar.copy, ON_SCALAR[1], 768, 896)
+        interleave(nc.scalar.copy, ON_SCALAR[1], 896, 1024)
         for i, parts in enumerate(STORES):
             start = parts[0][0]
             for a, b in parts:

@@ -17,9 +17,10 @@ COPY = mybir.ActivationFunctionType.Copy
 
 P = 128
 PACK = 4
-CAST_SPLIT = 108
-LATE = 128
+CAST_SPLIT = 80
+LATE = 512
 LEAD = 128
+SHARE = 192
 ON_VECTOR = ((0, 256), (256, 576))
 ON_SCALAR = ((576, 768), (768, 1024))
 STORES = (((0, 256), (256, 512)), ((512, 768),), ((768, 896), (896, 1024)))
@@ -45,7 +46,7 @@ def tile_picked_widxput_add_lo_kernel(tc, x_words, x_scales, mem, w1, slot, out_
         x_codes = keep.tile([P, T], U32, name="x_codes", align_bytes=64)
         x_plane = keep.tile([P, T], U8, name="x_plane", align_bytes=64)
         w_plane = keep.tile([P, N], U8, name="w_plane", align_bytes=64)
-        w_raw = [keep.tile([P, PACK, N // 2], F32, name=f"w_raw{h}", align_bytes=64) for h in range(2)]
+        w_raw = keep.tile([P, PACK, N], F32, name="w_raw", align_bytes=64)
         w_grouped = keep.tile([P, N * PACK], BF16, name="w_grouped", align_bytes=64)
         w_codes = keep.tile([P, N], U32, name="w_codes", align_bytes=64)
         store = [keep.tile([P, U], F32, name=f"store{t}") for t in range(PACK)]
@@ -63,9 +64,8 @@ def tile_picked_widxput_add_lo_kernel(tc, x_words, x_scales, mem, w1, slot, out_
             nc.sync.dma_start(out=store[t][:, a:b], in_=mem_rows[:, t, a:b])
 
         nc.vector.memset(x_plane[:].bitcast(I32), 0)
-        for h in range(2):
-            nc.sync.dma_start(out=w_raw[h][:], in_=w_rows[:, :, h * (N // 2) : (h + 1) * (N // 2)])
         nc.sync.dma_start(offsets[:], slot)
+        nc.sync.dma_start(out=w_raw[:], in_=w_rows)
         load_mem(0, 0, U)
         for q in range(4):
             nc.sync.dma_start(out=x_plane[32 * q : 32 * q + 4, :].bitcast(I32), in_=x_scale_rows[4 * q : 4 * q + 4, :])
@@ -77,17 +77,23 @@ def tile_picked_widxput_add_lo_kernel(tc, x_words, x_scales, mem, w1, slot, out_
         load_mem(3, U - LATE, U)
 
         acc = {}
+        for t in (0, 1):
+            for a, b in (front, back):
+                bank = psum.tile([P, half], F32, name=f"acc{t}_{a}")
+                acc[t, a, b] = bank[:]
+        for t in (2, 3):
+            bank = psum.tile([P, T], F32, name=f"acc{t}")
+            for a, b in (front, back, (0, T), (0, LEAD), (LEAD, T)):
+                acc[t, a, b] = bank[:, a:b]
 
-        def cast(copy, a, b):
-            h = a // (P // 2)
+        def cast(copy, pair, a, b):
             dealt = w_grouped[:].rearrange("p (t m j) -> p m j t", t=PACK, j=PACK)
-            raw = w_raw[h][:].rearrange("p j (m t) -> p m j t", t=PACK)
-            copy(out=dealt[:, a:b], in_=raw[:, a - h * (P // 2) : b - h * (P // 2)])
+            raw = w_raw[:].rearrange("p j (m t) -> p m j t", t=PACK)
+            copy(out=dealt[:, a:b, :, 2 * pair : 2 * pair + 2], in_=raw[:, a:b, :, 2 * pair : 2 * pair + 2])
 
         def multiply(t, a, b):
-            acc[t, a] = psum.tile([P, b - a], F32, name=f"acc{t}_{a}")
             nc.tensor.matmul_mx(
-                out=acc[t, a][:],
+                out=acc[t, a, b],
                 lhsT=w_codes[:, t * P : (t + 1) * P].bitcast(FP8X4),
                 lhsT_scale=w_plane[:, t * P : (t + 1) * P],
                 rhs=x_codes[:, a:b].bitcast(FP8X4),
@@ -102,14 +108,14 @@ def tile_picked_widxput_add_lo_kernel(tc, x_words, x_scales, mem, w1, slot, out_
         def gather_on_scalar(t, a, b):
             nc.scalar.activation(old[t][:, a:b], picked(t, a, b), COPY)
 
-        def add(t, a, b, sums):
-            nc.vector.tensor_tensor(fresh[t][:, a:b], old[t][:, a:b], sums, ADD)
+        def add(t, a, b):
+            nc.vector.tensor_tensor(fresh[t][:, a:b], old[t][:, a:b], acc[t, a, b], ADD)
 
         def scatter_on_scalar(t, a, b):
             nc.scalar.activation(picked(t, a, b), fresh[t][:, a:b], COPY)
 
         def fetch(copy, t, a, b):
-            copy(out=fresh[t][:, a:b], in_=acc[t, a][:])
+            copy(out=fresh[t][:, a:b], in_=acc[t, a, b])
 
         def scatter_sum(t):
             nc.vector.tensor_tensor(picked(t, 0, T), old[t][:], fresh[t][:], ADD)
@@ -128,37 +134,37 @@ def tile_picked_widxput_add_lo_kernel(tc, x_words, x_scales, mem, w1, slot, out_
                 in_=stage[part][:, :, a - first : b - first].rearrange("p t (c i) -> p c t i", i=4),
             )
 
-        cast(nc.vector.tensor_copy, 0, P // 2)
-        cast(nc.vector.tensor_copy, P // 2, CAST_SPLIT)
-        cast(nc.scalar.copy, CAST_SPLIT, P)
-        nc.vector.quantize_mx(out=w_codes[:].bitcast(FP8X4), scales=w_plane[:], in_=w_grouped[:])
+        cast(nc.vector.tensor_copy, 0, 0, P)
+        cast(nc.vector.tensor_copy, 1, CAST_SPLIT, P)
+        cast(nc.scalar.copy, 1, 0, CAST_SPLIT)
+        for a, b in ((0, N // 2), (N // 2, N)):
+            nc.vector.quantize_mx(out=w_codes[:, a:b].bitcast(FP8X4), scales=w_plane[:, a:b], in_=w_grouped[:, PACK * a : PACK * b])
 
         for t in (0, 1, 3, 2):
             multiply(t, *front)
-        for t in (1, 0, 3, 2):
+        for t in (1, 3, 0, 2):
             multiply(t, *back)
 
         gather_on_scalar(0, *front)
         gather_on_scalar(0, *back)
-        add(0, *front, acc[0, 0][:])
-        fetch(nc.scalar.copy, 1, *front)
+        add(0, *front)
         scatter_on_scalar(0, *front)
-        fetch(nc.vector.tensor_copy, 3, *front)
+        fetch(nc.vector.tensor_copy, 1, *front)
         nc.vector.tensor_copy(old[1][:], picked(1, 0, T))
-        fetch(nc.scalar.copy, 1, *back)
-        add(0, *back, acc[0, half][:])
+        fetch(nc.vector.tensor_copy, 1, *back)
+        fetch(nc.scalar.copy, 3, 0, T)
+        add(0, *back)
         scatter_on_scalar(0, *back)
-        fetch(nc.vector.tensor_copy, 3, *back)
         scatter_sum(1)
         for t in range(2):
             for part in stage:
                 move(nc.sync.dma_start, t, part)
             hand_on(t)
         gather_on_scalar(2, 0, T)
-        gather_on_scalar(3, 0, T)
-        add(2, 0, LEAD, acc[2, 0][:, 0:LEAD])
-        add(2, LEAD, half, acc[2, 0][:, LEAD:half])
-        add(2, *back, acc[2, half][:])
+        gather_on_scalar(3, 0, T - SHARE)
+        nc.vector.tensor_copy(old[3][:, T - SHARE : T], picked(3, T - SHARE, T))
+        add(2, 0, LEAD)
+        add(2, LEAD, T)
         scatter_on_scalar(2, 0, LEAD)
         scatter_on_scalar(2, LEAD, T)
         scatter_sum(3)

@@ -20,7 +20,7 @@ PACK = 4
 CAST_SPLIT = 80
 LATE = 512
 LEAD = 128
-SHARE = 192
+SHARE = 128
 ON_VECTOR = ((0, 256), (256, 576))
 ON_SCALAR = ((576, 768), (768, 1024))
 STORES = (((0, 256), (256, 512)), ((512, 768),), ((768, 896), (896, 1024)))
@@ -64,8 +64,8 @@ def tile_picked_widxput_add_lo_kernel(tc, x_words, x_scales, mem, w1, slot, out_
             nc.sync.dma_start(out=store[t][:, a:b], in_=mem_rows[:, t, a:b])
 
         nc.vector.memset(x_plane[:].bitcast(I32), 0)
-        nc.sync.dma_start(offsets[:], slot)
         nc.sync.dma_start(out=w_raw[:], in_=w_rows)
+        nc.sync.dma_start(offsets[:], slot)
         load_mem(0, 0, U)
         for q in range(4):
             nc.sync.dma_start(out=x_plane[32 * q : 32 * q + 4, :].bitcast(I32), in_=x_scale_rows[4 * q : 4 * q + 4, :])
@@ -77,14 +77,13 @@ def tile_picked_widxput_add_lo_kernel(tc, x_words, x_scales, mem, w1, slot, out_
         load_mem(3, U - LATE, U)
 
         acc = {}
-        for t in (0, 1):
+        for t in (0, 1, 3):
             for a, b in (front, back):
                 bank = psum.tile([P, half], F32, name=f"acc{t}_{a}")
                 acc[t, a, b] = bank[:]
-        for t in (2, 3):
-            bank = psum.tile([P, T], F32, name=f"acc{t}")
-            for a, b in (front, back, (0, T), (0, LEAD), (LEAD, T)):
-                acc[t, a, b] = bank[:, a:b]
+        bank = psum.tile([P, T], F32, name="acc2")
+        for a, b in (front, back, (0, LEAD), (LEAD, T)):
+            acc[2, a, b] = bank[:, a:b]
 
         def cast(copy, pair, a, b):
             dealt = w_grouped[:].rearrange("p (t m j) -> p m j t", t=PACK, j=PACK)
@@ -130,8 +129,8 @@ def tile_picked_widxput_add_lo_kernel(tc, x_words, x_scales, mem, w1, slot, out_
         def interleave(copy, part, a, b):
             first = part[0]
             copy(
-                out=grouped[:, PACK * a : PACK * b].rearrange("p (c i t) -> p c t i", i=4, t=PACK),
-                in_=stage[part][:, :, a - first : b - first].rearrange("p t (c i) -> p c t i", i=4),
+                out=grouped[:, PACK * a : PACK * b].rearrange("p (c i t) -> p c t i", i=2, t=PACK),
+                in_=stage[part][:, :, a - first : b - first].rearrange("p t (c i) -> p c t i", i=2),
             )
 
         cast(nc.vector.tensor_copy, 0, 0, P)
@@ -148,11 +147,12 @@ def tile_picked_widxput_add_lo_kernel(tc, x_words, x_scales, mem, w1, slot, out_
         gather_on_scalar(0, *front)
         gather_on_scalar(0, *back)
         add(0, *front)
+        fetch(nc.scalar.copy, 1, *front)
         scatter_on_scalar(0, *front)
-        fetch(nc.vector.tensor_copy, 1, *front)
+        fetch(nc.vector.tensor_copy, 3, *front)
         nc.vector.tensor_copy(old[1][:], picked(1, 0, T))
         fetch(nc.vector.tensor_copy, 1, *back)
-        fetch(nc.scalar.copy, 3, 0, T)
+        fetch(nc.scalar.copy, 3, *back)
         add(0, *back)
         scatter_on_scalar(0, *back)
         scatter_sum(1)

@@ -20,7 +20,8 @@ PACK = 4
 CAST_SPLIT = 80
 LATE = 512
 LEAD = 128
-SHARE = 128
+SHARE = 160
+TURN = 384
 ON_VECTOR = ((0, 256), (256, 576))
 ON_SCALAR = ((576, 768), (768, 1024))
 STORES = (((0, 256), (256, 512)), ((512, 768),), ((768, 896), (896, 1024)))
@@ -50,7 +51,9 @@ def tile_picked_widxput_add_lo_kernel(tc, x_words, x_scales, mem, w1, slot, out_
         w_grouped = keep.tile([P, N * PACK], BF16, name="w_grouped", align_bytes=64)
         w_codes = keep.tile([P, N], U32, name="w_codes", align_bytes=64)
         store = [keep.tile([P, U], F32, name=f"store{t}") for t in range(PACK)]
-        old = [keep.tile([P, T], F32, name=f"old{t}") for t in range(PACK)]
+        line = keep.tile([P, LEAD // 2 + T], F32, name="line")
+        old = [line[:, LEAD // 2 :] if t == 2 else keep.tile([P, T], F32, name=f"old{t}")[:] for t in range(PACK)]
+        turn = line[:, 0 : T - TURN]
         fresh = [keep.tile([P, T], F32, name=f"fresh{t}") for t in range(PACK)]
         stage = {(a, b): keep.tile([P, PACK, b - a], F32, name=f"stage{a}", align_bytes=64) for a, b in ON_VECTOR + ON_SCALAR}
         grouped = keep.tile([P, U * PACK], BF16, name="grouped", align_bytes=64)
@@ -82,8 +85,10 @@ def tile_picked_widxput_add_lo_kernel(tc, x_words, x_scales, mem, w1, slot, out_
                 bank = psum.tile([P, half], F32, name=f"acc{t}_{a}")
                 acc[t, a, b] = bank[:]
         bank = psum.tile([P, T], F32, name="acc2")
-        for a, b in (front, back, (0, LEAD), (LEAD, T)):
+        for a, b in ((0, LEAD // 2), (LEAD // 2, LEAD), front, back, (LEAD, T)):
             acc[2, a, b] = bank[:, a:b]
+        acc[1, half, TURN] = acc[1, half, T][:, 0 : TURN - half]
+        acc[1, TURN, T] = acc[1, half, T][:, TURN - half : half]
 
         def cast(copy, pair, a, b):
             dealt = w_grouped[:].rearrange("p (t m j) -> p m j t", t=PACK, j=PACK)
@@ -116,8 +121,8 @@ def tile_picked_widxput_add_lo_kernel(tc, x_words, x_scales, mem, w1, slot, out_
         def fetch(copy, t, a, b):
             copy(out=fresh[t][:, a:b], in_=acc[t, a, b])
 
-        def scatter_sum(t):
-            nc.vector.tensor_tensor(picked(t, 0, T), old[t][:], fresh[t][:], ADD)
+        def scatter_sum(t, a, b):
+            nc.vector.tensor_tensor(picked(t, a, b), old[t][:, a:b], fresh[t][:, a:b], ADD)
 
         def hand_on(t):
             nc.sync.dma_start(out=out_rows[:, t, :], in_=store[t][:])
@@ -150,24 +155,30 @@ def tile_picked_widxput_add_lo_kernel(tc, x_words, x_scales, mem, w1, slot, out_
         fetch(nc.scalar.copy, 1, *front)
         scatter_on_scalar(0, *front)
         fetch(nc.vector.tensor_copy, 3, *front)
-        nc.vector.tensor_copy(old[1][:], picked(1, 0, T))
-        fetch(nc.vector.tensor_copy, 1, *back)
+        nc.vector.tensor_copy(old[1], picked(1, 0, T))
+        fetch(nc.vector.tensor_copy, 1, half, TURN)
         fetch(nc.scalar.copy, 3, *back)
         add(0, *back)
         scatter_on_scalar(0, *back)
-        scatter_sum(1)
-        for t in range(2):
-            for part in stage:
-                move(nc.sync.dma_start, t, part)
-            hand_on(t)
-        gather_on_scalar(2, 0, T)
-        gather_on_scalar(3, 0, T - SHARE)
-        nc.vector.tensor_copy(old[3][:, T - SHARE : T], picked(3, T - SHARE, T))
-        add(2, 0, LEAD)
+        scatter_sum(1, 0, TURN)
+        for part in stage:
+            move(nc.sync.dma_start, 0, part)
+        hand_on(0)
+        gather_on_scalar(2, 0, LEAD)
+        gather_on_scalar(2, LEAD, T)
+        gather_on_scalar(3, 0, SHARE)
+        add(2, 0, LEAD // 2)
+        add(2, LEAD // 2, LEAD)
+        nc.vector.tensor_tensor(turn, old[1][:, TURN:T], acc[1, TURN, T], ADD)
+        nc.vector.tensor_copy(old[3][:, SHARE:T], picked(3, SHARE, T))
         add(2, LEAD, T)
         scatter_on_scalar(2, 0, LEAD)
+        nc.scalar.activation(picked(1, TURN, T), turn, COPY)
+        for part in stage:
+            move(nc.sync.dma_start, 1, part)
+        hand_on(1)
         scatter_on_scalar(2, LEAD, T)
-        scatter_sum(3)
+        scatter_sum(3, 0, T)
         hand_on(3)
         hand_on(2)
         for t in (3, 2):

@@ -22,6 +22,7 @@ LATE = 512
 LEAD = 128
 SHARE = 160
 TURN = 384
+SPARE = 96
 ON_VECTOR = ((0, 256), (256, 576))
 ON_SCALAR = ((576, 768), (768, 1024))
 STORES = (((0, 256), (256, 512)), ((512, 768),), ((768, 896), (896, 1024)))
@@ -51,8 +52,8 @@ def tile_picked_widxput_add_lo_kernel(tc, x_words, x_scales, mem, w1, slot, out_
         w_grouped = keep.tile([P, N * PACK], BF16, name="w_grouped", align_bytes=64)
         w_codes = keep.tile([P, N], U32, name="w_codes", align_bytes=64)
         store = [keep.tile([P, U], F32, name=f"store{t}") for t in range(PACK)]
-        line = keep.tile([P, LEAD // 2 + T], F32, name="line")
-        old = [line[:, LEAD // 2 :] if t == 2 else keep.tile([P, T], F32, name=f"old{t}")[:] for t in range(PACK)]
+        line = keep.tile([P, SPARE + T], F32, name="line")
+        old = [line[:, SPARE:] if t == 2 else keep.tile([P, T], F32, name=f"old{t}")[:] for t in range(PACK)]
         turn = line[:, 0 : T - TURN]
         fresh = [keep.tile([P, T], F32, name=f"fresh{t}") for t in range(PACK)]
         stage = {(a, b): keep.tile([P, PACK, b - a], F32, name=f"stage{a}", align_bytes=64) for a, b in ON_VECTOR + ON_SCALAR}
@@ -88,7 +89,9 @@ def tile_picked_widxput_add_lo_kernel(tc, x_words, x_scales, mem, w1, slot, out_
         for a, b in ((0, LEAD // 2), (LEAD // 2, LEAD), front, back, (LEAD, T)):
             acc[2, a, b] = bank[:, a:b]
         acc[1, half, TURN] = acc[1, half, T][:, 0 : TURN - half]
-        acc[1, TURN, T] = acc[1, half, T][:, TURN - half : half]
+        bank = psum.tile([P, T - TURN], F32, name="acc1_turn")
+        for a, b in ((TURN, T), (TURN, TURN + SPARE), (TURN + SPARE, T)):
+            acc[1, a, b] = bank[:, a - TURN : b - TURN]
 
         def cast(copy, pair, a, b):
             dealt = w_grouped[:].rearrange("p (t m j) -> p m j t", t=PACK, j=PACK)
@@ -124,6 +127,9 @@ def tile_picked_widxput_add_lo_kernel(tc, x_words, x_scales, mem, w1, slot, out_
         def scatter_sum(t, a, b):
             nc.vector.tensor_tensor(picked(t, a, b), old[t][:, a:b], fresh[t][:, a:b], ADD)
 
+        def add_turn(a, b):
+            nc.vector.tensor_tensor(turn[:, a - TURN : b - TURN], old[1][:, a:b], acc[1, a, b], ADD)
+
         def hand_on(t):
             nc.sync.dma_start(out=out_rows[:, t, :], in_=store[t][:])
 
@@ -146,8 +152,11 @@ def tile_picked_widxput_add_lo_kernel(tc, x_words, x_scales, mem, w1, slot, out_
 
         for t in (0, 1, 3, 2):
             multiply(t, *front)
-        for t in (1, 3, 0, 2):
-            multiply(t, *back)
+        multiply(1, half, TURN)
+        multiply(0, *back)
+        multiply(3, *back)
+        multiply(1, TURN, T)
+        multiply(2, *back)
 
         gather_on_scalar(0, *front)
         gather_on_scalar(0, *back)
@@ -160,6 +169,7 @@ def tile_picked_widxput_add_lo_kernel(tc, x_words, x_scales, mem, w1, slot, out_
         fetch(nc.scalar.copy, 3, *back)
         add(0, *back)
         scatter_on_scalar(0, *back)
+        add_turn(TURN, TURN + SPARE)
         scatter_sum(1, 0, TURN)
         for part in stage:
             move(nc.sync.dma_start, 0, part)
@@ -169,7 +179,7 @@ def tile_picked_widxput_add_lo_kernel(tc, x_words, x_scales, mem, w1, slot, out_
         gather_on_scalar(3, 0, SHARE)
         add(2, 0, LEAD // 2)
         add(2, LEAD // 2, LEAD)
-        nc.vector.tensor_tensor(turn, old[1][:, TURN:T], acc[1, TURN, T], ADD)
+        add_turn(TURN + SPARE, T)
         nc.vector.tensor_copy(old[3][:, SHARE:T], picked(3, SHARE, T))
         add(2, LEAD, T)
         scatter_on_scalar(2, 0, LEAD)

@@ -23,9 +23,10 @@ LEAD = 128
 SHARE = 160
 TURN = 384
 SPARE = 96
+HELD = 32
 ON_VECTOR = ((0, 256), (256, 576))
 ON_SCALAR = ((576, 768), (768, 1024))
-STORES = (((0, 256), (256, 512)), ((512, 768),), ((768, 896), (896, 1024)))
+STORES = (((0, 256), (256, 384)), ((384, 768),), ((768, 896), (896, 1024)))
 
 
 def tile_picked_widxput_add_lo_kernel(tc, x_words, x_scales, mem, w1, slot, out_0, out_1, out_2):
@@ -86,7 +87,7 @@ def tile_picked_widxput_add_lo_kernel(tc, x_words, x_scales, mem, w1, slot, out_
                 bank = psum.tile([P, half], F32, name=f"acc{t}_{a}")
                 acc[t, a, b] = bank[:]
         bank = psum.tile([P, T], F32, name="acc2")
-        for a, b in ((0, LEAD // 2), (LEAD // 2, LEAD), front, back, (LEAD, T)):
+        for a, b in ((0, HELD), (HELD, LEAD), front, back, (LEAD, T)):
             acc[2, a, b] = bank[:, a:b]
         acc[1, half, TURN] = acc[1, half, T][:, 0 : TURN - half]
         bank = psum.tile([P, T - TURN], F32, name="acc1_turn")
@@ -177,8 +178,8 @@ def tile_picked_widxput_add_lo_kernel(tc, x_words, x_scales, mem, w1, slot, out_
         gather_on_scalar(2, 0, LEAD)
         gather_on_scalar(2, LEAD, T)
         gather_on_scalar(3, 0, SHARE)
-        add(2, 0, LEAD // 2)
-        add(2, LEAD // 2, LEAD)
+        add(2, 0, HELD)
+        add(2, HELD, LEAD)
         add_turn(TURN + SPARE, T)
         nc.vector.tensor_copy(old[3][:, SHARE:T], picked(3, SHARE, T))
         add(2, LEAD, T)

from contextlib import ExitStack

import concourse.mybir as mybir

K, T, N, U = 512, 512, 512, 1024
FLOPS = 2 * K * T * N

F32 = mybir.dt.float32
BF16 = mybir.dt.bfloat16
I32 = mybir.dt.int32
U32 = mybir.dt.uint32
U16 = mybir.dt.uint16
U8 = mybir.dt.uint8
FP8X4 = mybir.dt.float8_e4m3fn_x4
ADD = mybir.AluOpType.add
COPY = mybir.ActivationFunctionType.Copy

P = 128
PACK = 4
CAST_SPLIT = 80
LATE = 512
LEAD = 128
SHARE = 160
TURN = 384
SPARE = 96
HELD = 32
ON_VECTOR = ((0, 256), (256, 576))
ON_SCALAR = ((576, 768), (768, 1024))
STORES = (((0, 256), (256, 384)), ((384, 768),), ((768, 896), (896, 1024)))


def tile_picked_widxput_add_lo_kernel(tc, x_words, x_scales, mem, w1, slot, out_0, out_1, out_2):
    nc = tc.nc
    mem_rows = mem.rearrange("(p t) u -> p t u", t=PACK)
    out_rows = out_0.rearrange("(p t) u -> p t u", t=PACK)
    w_rows = w1.rearrange("(p j) n -> p j n", j=PACK)
    x_rows = x_words[0].rearrange("p n r -> p (n r)").bitcast(I32)
    out_words = out_1[0].rearrange("p u r -> p (u r)").bitcast(I32)
    out_scales = out_2[0].bitcast(I32)
    x_scale_rows = x_scales[0].bitcast(I32)
    half = T // 2
    front, back = (0, half), (half, T)

    with ExitStack() as ctx:
        keep = ctx.enter_context(tc.tile_pool(name="keep", bufs=1))
        psum = ctx.enter_context(tc.psum_pool(name="psum", bufs=1))

        offsets = keep.tile([P, T // 16], U16, name="offsets")
        x_codes = keep.tile([P, T], U32, name="x_codes", align_bytes=64)
        x_plane = keep.tile([P, T], U8, name="x_plane", align_bytes=64)
        w_plane = keep.tile([P, N], U8, name="w_plane", align_bytes=64)
        w_raw = keep.tile([P, PACK, N], F32, name="w_raw", align_bytes=64)
        w_grouped = keep.tile([P, N * PACK], BF16, name="w_grouped", align_bytes=64)
        w_codes = keep.tile([P, N], U32, name="w_codes", align_bytes=64)
        store = [keep.tile([P, U], F32, name=f"store{t}") for t in range(PACK)]
        line = keep.tile([P, SPARE + T], F32, name="line")
        old = [line[:, SPARE:] if t == 2 else keep.tile([P, T], F32, name=f"old{t}")[:] for t in range(PACK)]
        turn = line[:, 0 : T - TURN]
        fresh = [keep.tile([P, T], F32, name=f"fresh{t}") for t in range(PACK)]
        stage = {(a, b): keep.tile([P, PACK, b - a], F32, name=f"stage{a}", align_bytes=64) for a, b in ON_VECTOR + ON_SCALAR}
        grouped = keep.tile([P, U * PACK], BF16, name="grouped", align_bytes=64)
        codes = [keep.tile([P, parts[-1][1] - parts[0][0]], U32, name=f"codes{parts[0][0]}", align_bytes=64) for parts in STORES]
        plane = keep.tile([P, U], U8, name="plane", align_bytes=64)

        def load_x(a, b):
            nc.sync.dma_start(out=x_codes[:, a:b].bitcast(I32), in_=x_rows[:, a:b])

        def load_mem(t, a, b):
            nc.sync.dma_start(out=store[t][:, a:b], in_=mem_rows[:, t, a:b])

        nc.vector.memset(x_plane[:].bitcast(I32), 0)
        nc.sync.dma_start(out=w_raw[:], in_=w_rows)
        nc.sync.dma_start(offsets[:], slot)
        load_mem(0, 0, U)
        for q in range(4):
            nc.sync.dma_start(out=x_plane[32 * q : 32 * q + 4, :].bitcast(I32), in_=x_scale_rows[4 * q : 4 * q + 4, :])
        load_x(*front)
        load_mem(1, 0, U)
        load_x(*back)
        load_mem(3, 0, U - LATE)
        load_mem(2, 0, U)
        load_mem(3, U - LATE, U)

        acc = {}
        for t in (0, 1, 3):
            for a, b in (front, back):
                bank = psum.tile([P, half], F32, name=f"acc{t}_{a}")
                acc[t, a, b] = bank[:]
        bank = psum.tile([P, T], F32, name="acc2")
        for a, b in ((0, HELD), (HELD, LEAD), front, back, (LEAD, T)):
            acc[2, a, b] = bank[:, a:b]
        acc[1, half, TURN] = acc[1, half, T][:, 0 : TURN - half]
        bank = psum.tile([P, T - TURN], F32, name="acc1_turn")
        for a, b in ((TURN, T), (TURN, TURN + SPARE), (TURN + SPARE, T)):
            acc[1, a, b] = bank[:, a - TURN : b - TURN]

        def cast(copy, pair, a, b):
            dealt = w_grouped[:].rearrange("p (t m j) -> p m j t", t=PACK, j=PACK)
            raw = w_raw[:].rearrange("p j (m t) -> p m j t", t=PACK)
            copy(out=dealt[:, a:b, :, 2 * pair : 2 * pair + 2], in_=raw[:, a:b, :, 2 * pair : 2 * pair + 2])

        def multiply(t, a, b):
            nc.tensor.matmul_mx(
                out=acc[t, a, b],
                lhsT=w_codes[:, t * P : (t + 1) * P].bitcast(FP8X4),
                lhsT_scale=w_plane[:, t * P : (t + 1) * P],
                rhs=x_codes[:, a:b].bitcast(FP8X4),
                rhs_scale=x_plane[:, a:b],
                start=True,
                stop=True,
            )

        def picked(t, a, b):
            return store[t][:].indirect(offsets[:, a // 16 : b // 16])

        def gather_on_scalar(t, a, b):
            nc.scalar.activation(old[t][:, a:b], picked(t, a, b), COPY)

        def add(t, a, b):
            nc.vector.tensor_tensor(fresh[t][:, a:b], old[t][:, a:b], acc[t, a, b], ADD)

        def scatter_on_scalar(t, a, b):
            nc.scalar.activation(picked(t, a, b), fresh[t][:, a:b], COPY)

        def fetch(copy, t, a, b):
            copy(out=fresh[t][:, a:b], in_=acc[t, a, b])

        def scatter_sum(t, a, b):
            nc.vector.tensor_tensor(picked(t, a, b), old[t][:, a:b], fresh[t][:, a:b], ADD)

        def add_turn(a, b):
            nc.vector.tensor_tensor(turn[:, a - TURN : b - TURN], old[1][:, a:b], acc[1, a, b], ADD)

        def hand_on(t):
            nc.sync.dma_start(out=out_rows[:, t, :], in_=store[t][:])

        def move(copy, t, part):
            a, b = part
            copy(out=stage[part][:, t, :], in_=store[t][:, a:b])

        def interleave(copy, part, a, b):
            first = part[0]
            copy(
                out=grouped[:, PACK * a : PACK * b].rearrange("p (c i t) -> p c t i", i=2, t=PACK),
                in_=stage[part][:, :, a - first : b - first].rearrange("p t (c i) -> p c t i", i=2),
            )

        cast(nc.vector.tensor_copy, 0, 0, P)
        cast(nc.vector.tensor_copy, 1, CAST_SPLIT, P)
        cast(nc.scalar.copy, 1, 0, CAST_SPLIT)
        for a, b in ((0, N // 2), (N // 2, N)):
            nc.vector.quantize_mx(out=w_codes[:, a:b].bitcast(FP8X4), scales=w_plane[:, a:b], in_=w_grouped[:, PACK * a : PACK * b])

        for t in (0, 1, 3, 2):
            multiply(t, *front)
        multiply(1, half, TURN)
        multiply(0, *back)
        multiply(3, *back)
        multiply(1, TURN, T)
        multiply(2, *back)

        gather_on_scalar(0, *front)
        gather_on_scalar(0, *back)
        add(0, *front)
        fetch(nc.scalar.copy, 1, *front)
        scatter_on_scalar(0, *front)
        fetch(nc.vector.tensor_copy, 3, *front)
        nc.vector.tensor_copy(old[1], picked(1, 0, T))
        fetch(nc.vector.tensor_copy, 1, half, TURN)
        fetch(nc.scalar.copy, 3, *back)
        add(0, *back)
        scatter_on_scalar(0, *back)
        add_turn(TURN, TURN + SPARE)
        scatter_sum(1, 0, TURN)
        for part in stage:
            move(nc.sync.dma_start, 0, part)
        hand_on(0)
        gather_on_scalar(2, 0, LEAD)
        gather_on_scalar(2, LEAD, T)
        gather_on_scalar(3, 0, SHARE)
        add(2, 0, HELD)
        add(2, HELD, LEAD)
        add_turn(TURN + SPARE, T)
        nc.vector.tensor_copy(old[3][:, SHARE:T], picked(3, SHARE, T))
        add(2, LEAD, T)
        scatter_on_scalar(2, 0, LEAD)
        nc.scalar.activation(picked(1, TURN, T), turn, COPY)
        for part in stage:
            move(nc.sync.dma_start, 1, part)
        hand_on(1)
        scatter_on_scalar(2, LEAD, T)
        scatter_sum(3, 0, T)
        hand_on(3)
        hand_on(2)
        for t in (3, 2):
            for part in ON_VECTOR:
                move(nc.vector.tensor_copy, t, part)
            for part in ON_SCALAR:
                move(nc.scalar.copy, t, part)

        for part in ON_VECTOR:
            interleave(nc.vector.tensor_copy, part, *part)
        interleave(nc.scalar.copy, ON_SCALAR[0], *ON_SCALAR[0])
        interleave(nc.scalar.copy, ON_SCALAR[1], 768, 896)
        interleave(nc.scalar.copy, ON_SCALAR[1], 896, 1024)
        for i, parts in enumerate(STORES):
            start = parts[0][0]
            for a, b in parts:
                nc.vector.quantize_mx(out=codes[i][:, a - start : b - start].bitcast(FP8X4), scales=plane[:, a:b], in_=grouped[:, PACK * a : PACK * b])
            nc.sync.dma_start(out=out_words[:, start : parts[-1][1]], in_=codes[i][:].bitcast(I32))
        for q in range(4):
            queue = nc.scalar if q % 2 else nc.sync
            queue.dma_start(out=out_scales[4 * q : 4 * q + 4, :], in_=plane[32 * q : 32 * q + 4, :].bitcast(I32))
